import numpy as np
import ml_dtypes


def mxq(x, axis, fmt="e4m3"):
    dtype, down = {"e4m3": (ml_dtypes.float8_e4m3fn, 7), "e5m2": (ml_dtypes.float8_e5m2, 14)}[fmt]
    v = np.moveaxis(np.asarray(x, np.float32).astype(ml_dtypes.bfloat16).astype(np.float64), axis, -1)
    blocks = v.reshape(v.shape[:-1] + (-1, 32))
    amax = np.abs(blocks).max(-1, keepdims=True)
    byte = np.maximum(np.where(amax > 0, np.frexp(amax)[1] - 1 + 127, 0) - down, 1)
    scale = np.exp2(byte - 127.0)
    codes = (blocks / scale).astype(np.float32).astype(dtype).astype(np.float64)
    return np.moveaxis((codes * scale).reshape(v.shape), -1, axis)


WIDE = False


def mx_kscale(k):
    if not WIDE:
        return np.ones(k)
    levels = np.array([10, -10, 5, -5, 0])
    if k % 512:
        return np.exp2(np.random.permutation(np.resize(levels, k // 32))).repeat(32)
    a = np.empty((k // 512, 16))
    for p in range(k // 512):
        a[p, :8] = np.random.permutation(np.resize(levels, 8))
        for g in range(8):
            far = levels[np.abs(levels - a[p, g]) >= 10]
            a[p, g + 8] = far[np.random.randint(len(far))]
    return np.exp2(a.ravel()).repeat(32)


def f64(x):
    return np.asarray(x).astype(np.float64)


def striped(idx):
    return np.tile(idx.reshape(-1, 16).T, (8, 1)).astype(np.uint16)


def unstriped(offs):
    return offs[:16].T.reshape(-1).astype(np.int64)


def pack_weight(w):
    k, n = w.shape
    w = f64(np.asarray(w, np.float32).astype(ml_dtypes.bfloat16)).reshape(k // 32, 32, n)
    amax = np.abs(w).max(1)
    byte = np.clip(np.where(amax > 0, np.frexp(amax)[1] - 1 + 127 - 7, 1), 1, 254)
    scaled = (w * np.exp2(127.0 - byte)[:, None, :]).reshape(k, n).astype(np.float32)
    words = np.ascontiguousarray(scaled.reshape(k // 512, 128, 4, n).transpose(0, 1, 3, 2)).astype(ml_dtypes.float8_e4m3fn).view(np.uint8)
    return words, np.ascontiguousarray(byte.astype(np.uint8).reshape(k // 512, 16, n))


def unpack_weight(words, scales):
    g, p, n, _ = words.shape
    vals = np.ascontiguousarray(words).view(ml_dtypes.float8_e4m3fn).astype(np.float64) * np.repeat(np.exp2(scales.astype(np.float64) - 127.0), 8, axis=1)[..., None]
    return vals.transpose(0, 1, 3, 2).reshape(g * 512, n)


K, T, S, N, H = 512, 1024, 512, 128, 512


def setup_inputs():
    n = np.random.standard_normal
    s = mx_kscale(K)[:, None]
    u = mx_kscale(H)
    packed_xT = pack_weight(n((K, T)) * s)
    return {
        "x_words": packed_xT[0],
        "x_scales": packed_xT[1],
        "w1": (n((K, H)) / np.sqrt(K) / s).astype(np.float32),
        "w2": (n((K, H)) / np.sqrt(K) / s).astype(np.float32),
        "unit": (np.random.uniform(0.6, 1.4, (H, 1)) * u[:, None]).astype(np.float32),
        "w3": (n((H, N)) / np.sqrt(H) / u[:, None]).astype(np.float32),
        "offs": striped(np.random.permutation(T)[:S]),
        "nxt": striped(np.random.permutation(S)),
        "prv": striped(np.random.permutation(S)),
    }


def reference(x_words, x_scales, w1, w2, unit, w3, offs, nxt, prv):
    xq = unpack_weight(x_words, x_scales)[:, unstriped(offs)]
    px = mxq(f64(w1), 0, "e4m3").T @ xq
    xnxt = px[:, unstriped(nxt)]
    dnxt = xnxt - px
    py = mxq(f64(w2), 0, "e4m3").T @ xq
    ynxt = py[:, unstriped(nxt)]
    enxt = ynxt - py
    r2 = (dnxt) ** 2 + (enxt) ** 2
    fene = dnxt / (-0.9 * (r2 / (r2 + 4.0)) + 1.0)
    xprv = px[:, unstriped(prv)]
    dprv = xprv - px
    yprv = py[:, unstriped(prv)]
    eprv = yprv - py
    dot = dnxt * dprv + enxt * eprv
    bend = dot * (dprv / (np.sqrt((dprv) ** 2 + (eprv) ** 2 + 0.1) + 0.3))
    hid = f64(unit) * (fene + 0.5 * bend)
    return mxq(f64(w3), 0, "e4m3").T @ mxq(hid, 0, "e4m3")

@@ -1,0 +1,222 @@
+from contextlib import ExitStack
+
+import concourse.mybir as mybir
+from concourse.masks import make_identity
+
+K, T, S, N, H = 512, 1024, 512, 128, 512
+FLOPS = 2 * K * H * S * 2 + 2 * H * N * S
+
+F32 = mybir.dt.float32
+BF16 = mybir.dt.bfloat16
+I32 = mybir.dt.int32
+U32 = mybir.dt.uint32
+U16 = mybir.dt.uint16
+U8 = mybir.dt.uint8
+FP8X4 = mybir.dt.float8_e4m3fn_x4
+ALU = mybir.AluOpType
+ACT = mybir.ActivationFunctionType
+
+P = 128
+PACK = 4
+PIECE = 256
+GROUPS = ((0, 1), (128, 1), (256, 2))
+
+
+def tile_picked_ypolym_force_p_kernel(
+    tc, x_words, x_scales, w1, w2, unit, w3, offs, nxt, prv, out
+):
+    nc = tc.nc
+    with ExitStack() as ctx:
+        keep = ctx.enter_context(tc.tile_pool(name="keep", bufs=1))
+        work = ctx.enter_context(tc.tile_pool(name="work", bufs=2))
+        psum = ctx.enter_context(tc.psum_pool(name="psum", bufs=8))
+
+        def new_bank():
+            return psum.tile([P, 512], F32, name="bank", tag="bank")
+
+        offs_sb = keep.tile([P, S // 16], U16, name="offs_sb")
+        nxt_sb = keep.tile([P, S // 16], U16, name="nxt_sb")
+        prv_sb = keep.tile([P, S // 16], U16, name="prv_sb")
+        all_scales = keep.tile([P, T], U8, name="all_scales", align_bytes=64)
+        all_words = keep.tile([P, T], U32, name="all_words", align_bytes=64)
+        nc.vector.memset(all_scales[:].bitcast(I32), 0)
+        nc.sync.dma_start(offs_sb[:], offs)
+        for q in range(4):
+            nc.sync.dma_start(
+                all_scales[32 * q : 32 * q + 4, :].bitcast(I32),
+                x_scales[0, 4 * q : 4 * q + 4, :].bitcast(I32),
+            )
+        nc.sync.dma_start(
+            all_words[:].bitcast(I32), x_words[0].rearrange("p n t -> p (n t)").bitcast(I32)
+        )
+
+        def load_w(w, c0, width, name):
+            raw = keep.tile([P, PACK, width], F32, name=name)
+            nc.sync.dma_start(raw[:], w[:, c0 : c0 + width].rearrange("(p j) c -> p j c", j=PACK))
+            return raw
+
+        raws = {}
+        for gi, (c0, g) in enumerate(GROUPS):
+            raws[gi] = (load_w(w1, c0, P * g, "w1_raw%d" % gi), load_w(w2, c0, P * g, "w2_raw%d" % gi))
+            if gi == 0:
+                nc.sync.dma_start(nxt_sb[:], nxt)
+                nc.sync.dma_start(prv_sb[:], prv)
+        w3_raw = load_w(w3, 0, N, "w3_raw")
+        unit_sb = keep.tile([P, PACK], F32, name="unit_sb")
+        nc.sync.dma_start(unit_sb[:], unit.rearrange("(p t) o -> p (t o)", t=PACK))
+        lists = (nxt_sb, prv_sb)
+
+        ident = keep.tile([P, P], F32, name="ident")
+        make_identity(nc, ident[:])
+
+        x_bytes = keep.tile([P, S], U8, name="x_bytes", align_bytes=64)
+        x_codes = keep.tile([P, S], U32, name="x_codes", align_bytes=64)
+        nc.vector.tensor_copy(x_bytes[:], all_scales[:].indirect(offs_sb[:]))
+        nc.vector.tensor_copy(x_codes[:], all_words[:].indirect(offs_sb[:]))
+
+        def quantise(raw, width, dealt, name, on_scalar):
+            wb = keep.tile([P, width * PACK], BF16, name=name + "_bf", align_bytes=64)
+            if dealt:
+                dst = wb[:].rearrange("p (t m j) -> p m j t", t=PACK, j=PACK)
+                src = raw[:].rearrange("p j (m t) -> p m j t", t=PACK)
+            else:
+                dst = wb[:].rearrange("p (m t j) -> p m j t", t=PACK, j=PACK)
+                src = raw[:].rearrange("p j (m t) -> p m j t", t=PACK)
+            if on_scalar:
+                nc.scalar.copy(dst, src)
+            else:
+                nc.vector.tensor_copy(dst, src)
+            codes = keep.tile([P, width], U32, name=name + "_codes", align_bytes=64)
+            scales = keep.tile([P, width], U8, name=name + "_scales", align_bytes=64)
+            nc.vector.quantize_mx(out=codes[:].bitcast(FP8X4), scales=scales[:], in_=wb[:])
+            return codes, scales
+
+        def products(gi):
+            c0, g = GROUPS[gi]
+            xy = keep.tile([P, g, 2, S], F32, name="xy%d" % gi)
+            for c in range(2):
+                codes, scales = quantise(raws[gi][c], P * g, True, "w%d_%d" % (c, gi), gi == 0)
+                for pl in range(g):
+                    bank = new_bank()
+                    cols = slice(pl * P, (pl + 1) * P)
+                    nc.tensor.matmul_mx(
+                        out=bank[:], lhsT=codes[:, cols].bitcast(FP8X4), lhsT_scale=scales[:, cols],
+                        rhs=x_codes[:].bitcast(FP8X4), rhs_scale=x_bytes[:], start=True, stop=True,
+                    )
+                    nc.scalar.copy(xy[:, pl, c, :], bank[:])
+            return xy
+
+        fene_t = keep.tile([P, 16, P], F32, name="fene_t")
+        bend_t = keep.tile([P, 16, P], F32, name="bend_t")
+
+        def turn(bank, terms, g):
+            width = S // g
+            for jb in range(width // P):
+                for pl in range(g):
+                    dst = bank[:, (jb * g + pl) * P : (jb * g + pl + 1) * P]
+                    cols = slice(pl * width + jb * P, pl * width + (jb + 1) * P)
+                    for n, term in enumerate(terms):
+                        nc.tensor.matmul(
+                            dst, term[:, cols], ident[:], is_transpose=True,
+                            start=(n == 0), stop=(n == len(terms) - 1),
+                        )
+
+        def forces(gi, xy, j0):
+            c0, g = GROUPS[gi]
+            width = S // g
+            got = work.tile([P, 2, 2, S], F32, name="got")
+            diff = work.tile([P, 2, 2, S], F32, name="diff")
+            sq = work.tile([P, 2, 2, S], F32, name="sq")
+            for li in (1, 0):
+                for c in range(2):
+                    for pl in range(g):
+                        for s0 in range(0, width, PIECE):
+                            dst = got[:, li, c, pl * width + s0 : pl * width + s0 + PIECE]
+                            src = xy[:, pl, c, :].indirect(lists[li][:, (j0 + s0) // 16 : (j0 + s0 + PIECE) // 16])
+                            if c == 0:
+                                nc.vector.tensor_copy(dst, src)
+                            else:
+                                nc.scalar.activation(dst, src, ACT.Copy)
+                nc.vector.tensor_tensor(
+                    diff[:, li].rearrange("p c (g w) -> p c g w", g=g),
+                    xy[:, :, :, j0 : j0 + width].rearrange("p g c w -> p c g w"),
+                    got[:, li].rearrange("p c (g w) -> p c g w", g=g),
+                    ALU.subtract,
+                )
+                nc.scalar.activation(sq[:, li], diff[:, li], ACT.Square)
+            d, e, dp, ep = diff[:, 0, 0], diff[:, 0, 1], diff[:, 1, 0], diff[:, 1, 1]
+            q_bank = new_bank()
+            turn(q_bank, (sq[:, 1, 0], sq[:, 1, 1]), g)
+            r_bank = new_bank()
+            turn(r_bank, (sq[:, 0, 0], sq[:, 0, 1]), g)
+            d_bank = new_bank()
+            turn(d_bank, (d,), g)
+            n1 = work.tile([P, S], F32, name="n1")
+            n2 = work.tile([P, S], F32, name="n2")
+            n3 = work.tile([P, S], F32, name="n3")
+            nc.vector.tensor_tensor(n2[:], e, ep, ALU.mult)
+            nc.vector.tensor_tensor(n1[:], d, sq[:, 1, 0], ALU.mult)
+            nc.vector.tensor_tensor(n3[:], n2[:], dp, ALU.mult)
+            n_bank = new_bank()
+            turn(n_bank, (n1[:], n3[:]), g)
+
+            rho = work.tile([P, S], F32, name="rho")
+            den2 = work.tile([P, 2, S], F32, name="den2")
+            inv = work.tile([P, 2, S], F32, name="inv")
+            nc.scalar.activation(rho[:], q_bank[:], ACT.Abs_reciprocal_sqrt, bias=0.1)
+            nc.scalar.activation(den2[:, 0], r_bank[:], ACT.Square, scale=1.0 / 360.0, bias=1.0 / 9.0)
+            nc.scalar.activation(den2[:, 1], rho[:], ACT.Square, scale=0.18, bias=0.6)
+            nc.scalar.activation(inv[:, 0], den2[:, 0], ACT.Abs_reciprocal_sqrt)
+            nc.scalar.activation(inv[:, 1], den2[:, 1], ACT.Abs_reciprocal_sqrt)
+            rows = slice(j0 // P * PACK, (j0 + width) // P * PACK)
+            cols = slice(c0 // PACK, c0 // PACK + 32 * g)
+            for dst, k, const, bank in ((fene_t, 0, 10.0, d_bank), (bend_t, 1, 5.0 / 3.0, n_bank)):
+                nc.vector.scalar_tensor_tensor(
+                    dst[:, rows, cols],
+                    inv[:, k].rearrange("p (a m) -> p a m", m=32 * g),
+                    const,
+                    bank[:].rearrange("p (a m) -> p a m", m=32 * g),
+                    ALU.subtract,
+                    ALU.mult,
+                )
+
+        def observe(j0, width, w3_codes, w3_scales):
+            hid = work.tile([P, width, PACK], BF16, name="hid", align_bytes=64)
+            for jb in range(j0 // P, (j0 + width) // P):
+                bank = new_bank()
+                for t in range(PACK):
+                    for n, term in enumerate((fene_t, bend_t)):
+                        nc.tensor.matmul(
+                            bank[:, t * P : (t + 1) * P], term[:, jb * PACK + t, :], ident[:],
+                            is_transpose=True, start=(n == 0), stop=(n == 1),
+                        )
+                nc.vector.tensor_tensor(
+                    hid[:, jb * P - j0 : (jb + 1) * P - j0, :],
+                    bank[:].rearrange("p (t j) -> p j t", t=PACK),
+                    unit_sb[:].unsqueeze(1).to_broadcast([P, P, PACK]),
+                    ALU.mult,
+                )
+            codes = work.tile([P, width], U32, name="hid_codes", align_bytes=64)
+            scales = work.tile([P, width], U8, name="hid_scales", align_bytes=64)
+            nc.vector.quantize_mx(
+                out=codes[:].bitcast(FP8X4), scales=scales[:], in_=hid[:].rearrange("p j t -> p (j t)")
+            )
+            bank = new_bank()
+            nc.tensor.matmul_mx(
+                out=bank[:, :width], lhsT=w3_codes[:].bitcast(FP8X4), lhsT_scale=w3_scales[:],
+                rhs=codes[:].bitcast(FP8X4), rhs_scale=scales[:], start=True, stop=True,
+            )
+            res = work.tile([P, width], F32, name="res")
+            nc.scalar.copy(res[:], bank[:, :width])
+            nc.sync.dma_start(out[:, j0 : j0 + width], res[:])
+
+        xy0 = products(0)
+        xy1 = products(1)
+        forces(0, xy0, 0)
+        xy2 = products(2)
+        forces(1, xy1, 0)
+        w3_codes, w3_scales = quantise(w3_raw, N, False, "w3", False)
+        forces(2, xy2, 0)
+        observe(0, 256, w3_codes, w3_scales)
+        forces(2, xy2, 256)
+        observe(256, 256, w3_codes, w3_scales)

@@ -19,6 +19,7 @@ ACT = mybir.ActivationFunctionType
 P = 128
 PACK = 4
 PIECE = 256
+BANKS = {"mm":4,"qr":4}
 GROUPS = ((0, 1), (128, 1), (256, 2))
 
 
@@ -28,18 +29,18 @@ def tile_picked_ypolym_force_p_kernel(
     nc = tc.nc
     with ExitStack() as ctx:
         keep = ctx.enter_context(tc.tile_pool(name="keep", bufs=1))
-        work = ctx.enter_context(tc.tile_pool(name="work", bufs=2))
-        psum = ctx.enter_context(tc.psum_pool(name="psum", bufs=8))
+        work = ctx.enter_context(tc.tile_pool(name="work", bufs=3))
+        psum = ctx.enter_context(tc.psum_pool(name="psum", bufs=1))
 
-        def new_bank():
-            return psum.tile([P, 512], F32, name="bank", tag="bank")
+        def new_bank(tag):
+            return psum.tile([P, 512], F32, name=tag, tag=tag, bufs=BANKS[tag])
 
         offs_sb = keep.tile([P, S // 16], U16, name="offs_sb")
         nxt_sb = keep.tile([P, S // 16], U16, name="nxt_sb")
         prv_sb = keep.tile([P, S // 16], U16, name="prv_sb")
         all_scales = keep.tile([P, T], U8, name="all_scales", align_bytes=64)
         all_words = keep.tile([P, T], U32, name="all_words", align_bytes=64)
-        nc.vector.memset(all_scales[:].bitcast(I32), 0)
+        nc.gpsimd.memset(all_scales[:].bitcast(I32), 0)
         nc.sync.dma_start(offs_sb[:], offs)
         for q in range(4):
             nc.sync.dma_start(
@@ -59,8 +60,8 @@ def tile_picked_ypolym_force_p_kernel(
         for gi, (c0, g) in enumerate(GROUPS):
             raws[gi] = (load_w(w1, c0, P * g, "w1_raw%d" % gi), load_w(w2, c0, P * g, "w2_raw%d" % gi))
             if gi == 0:
-                nc.sync.dma_start(nxt_sb[:], nxt)
                 nc.sync.dma_start(prv_sb[:], prv)
+                nc.sync.dma_start(nxt_sb[:], nxt)
         w3_raw = load_w(w3, 0, N, "w3_raw")
         unit_sb = keep.tile([P, PACK], F32, name="unit_sb")
         nc.sync.dma_start(unit_sb[:], unit.rearrange("(p t) o -> p (t o)", t=PACK))
@@ -74,16 +75,17 @@ def tile_picked_ypolym_force_p_kernel(
         nc.vector.tensor_copy(x_bytes[:], all_scales[:].indirect(offs_sb[:]))
         nc.vector.tensor_copy(x_codes[:], all_words[:].indirect(offs_sb[:]))
 
-        def quantise(raw, width, dealt, name, on_scalar):
+        def quantise(raw, width, name, eng):
             wb = keep.tile([P, width * PACK], BF16, name=name + "_bf", align_bytes=64)
-            if dealt:
-                dst = wb[:].rearrange("p (t m j) -> p m j t", t=PACK, j=PACK)
-                src = raw[:].rearrange("p j (m t) -> p m j t", t=PACK)
-            else:
-                dst = wb[:].rearrange("p (m t j) -> p m j t", t=PACK, j=PACK)
-                src = raw[:].rearrange("p j (m t) -> p m j t", t=PACK)
-            if on_scalar:
+            dst = wb[:].rearrange("p (m t j) -> p m j t", t=PACK, j=PACK)
+            src = raw[:].rearrange("p j (m t) -> p m j t", t=PACK)
+            if eng == "S":
                 nc.scalar.copy(dst, src)
+            elif eng == "G":
+                nc.gpsimd.tensor_scalar(
+                    wb[:].rearrange("p (m j) -> p m j", j=PACK), raw[:].rearrange("p j m -> p m j"),
+                    1.0, 0.0, ALU.mult, ALU.add,
+                )
             else:
                 nc.vector.tensor_copy(dst, src)
             codes = keep.tile([P, width], U32, name=name + "_codes", align_bytes=64)
@@ -93,24 +95,34 @@ def tile_picked_ypolym_force_p_kernel(
 
         def products(gi):
             c0, g = GROUPS[gi]
-            xy = keep.tile([P, g, 2, S], F32, name="xy%d" % gi)
+            tables = [[], []]
+            plain = keep.tile([P, 2, g, S], F32, name="plain%d" % gi)
             for c in range(2):
-                codes, scales = quantise(raws[gi][c], P * g, True, "w%d_%d" % (c, gi), gi == 0)
+                codes, scales = quantise(raws[gi][c], P * g, "w%d_%d" % (c, gi), "SSVVVVVVV"[2 * gi + c])
                 for pl in range(g):
-                    bank = new_bank()
+                    bank = new_bank("mm")
                     cols = slice(pl * P, (pl + 1) * P)
                     nc.tensor.matmul_mx(
                         out=bank[:], lhsT=codes[:, cols].bitcast(FP8X4), lhsT_scale=scales[:, cols],
                         rhs=x_codes[:].bitcast(FP8X4), rhs_scale=x_bytes[:], start=True, stop=True,
                     )
-                    nc.scalar.copy(xy[:, pl, c, :], bank[:])
-            return xy
+                    if gi > 1 or c == 0:
+                        table = keep.tile([P, S], F32, name="table%d_%d_%d" % (gi, c, pl))
+                        nc.scalar.copy(table[:], bank[:])
+                        if gi == 0:
+                            nc.scalar.copy(plain[:, c, pl, :], bank[:])
+                        else:
+                            nc.sync.dma_start(plain[:, c, pl, :], table[:])
+                        tables[c].append(table[:])
+                    else:
+                        nc.scalar.copy(plain[:, c, pl, :], bank[:])
+                        tables[c].append(plain[:, c, pl, :])
+            return tables, plain
 
-        fene_t = keep.tile([P, 16, P], F32, name="fene_t")
-        bend_t = keep.tile([P, 16, P], F32, name="bend_t")
+        fene_t = keep.tile([P, 2, PACK, 2, P], F32, name="fene_t")
+        bend_t = keep.tile([P, 2, PACK, 2, P], F32, name="bend_t")
 
-        def turn(bank, terms, g):
-            width = S // g
+        def turn(bank, terms, g, width):
             for jb in range(width // P):
                 for pl in range(g):
                     dst = bank[:, (jb * g + pl) * P : (jb * g + pl + 1) * P]
@@ -120,80 +132,105 @@ def tile_picked_ypolym_force_p_kernel(
                             dst, term[:, cols], ident[:], is_transpose=True,
                             start=(n == 0), stop=(n == len(terms) - 1),
                         )
+            return bank[:, : g * width].rearrange("p (a t) -> p t a", t=PACK)
 
-        def forces(gi, xy, j0):
+        def by_slot(ap):
+            return ap.rearrange("p (t a) -> p t a", t=PACK)
+
+        def forces(gi, made, j0, width, lend):
+            tables, plain = made
             c0, g = GROUPS[gi]
-            width = S // g
-            got = work.tile([P, 2, 2, S], F32, name="got")
-            diff = work.tile([P, 2, 2, S], F32, name="diff")
-            sq = work.tile([P, 2, 2, S], F32, name="sq")
+            u = (gi, j0)
+            cols = g * width
+            piece = min(PIECE, width)
+            got = work.tile([P, 2, 2, cols], F32, name="got")
+            diff = work.tile([P, 2, 2, cols], F32, name="diff")
+            sq = work.tile([P, 2, 2, cols], F32, name="sq")
             for li in (1, 0):
+                rest = []
                 for c in range(2):
+                    fused = c == 0 or gi == 2
                     for pl in range(g):
-                        for s0 in range(0, width, PIECE):
-                            dst = got[:, li, c, pl * width + s0 : pl * width + s0 + PIECE]
-                            src = xy[:, pl, c, :].indirect(lists[li][:, (j0 + s0) // 16 : (j0 + s0 + PIECE) // 16])
-                            if c == 0:
-                                nc.vector.tensor_copy(dst, src)
+                        for s0 in range(0, width, piece):
+                            part = slice(pl * width + s0, pl * width + s0 + piece)
+                            src = tables[c][pl].indirect(lists[li][:, (j0 + s0) // 16 : (j0 + s0 + piece) // 16])
+                            if fused:
+                                nc.vector.tensor_tensor(
+                                    diff[:, li, c, part], src, plain[:, c, pl, j0 + s0 : j0 + s0 + piece], ALU.subtract
+                                )
+                            elif c == 0:
+                                nc.vector.tensor_copy(got[:, li, c, part], src)
                             else:
-                                nc.scalar.activation(dst, src, ACT.Copy)
-                nc.vector.tensor_tensor(
-                    diff[:, li].rearrange("p c (g w) -> p c g w", g=g),
-                    xy[:, :, :, j0 : j0 + width].rearrange("p g c w -> p c g w"),
-                    got[:, li].rearrange("p c (g w) -> p c g w", g=g),
-                    ALU.subtract,
-                )
-                nc.scalar.activation(sq[:, li], diff[:, li], ACT.Square)
+                                nc.scalar.activation(got[:, li, c, part], src, ACT.Copy)
+                    if not fused:
+                        rest.append(c)
+                if rest:
+                    cs = slice(rest[0], rest[-1] + 1)
+                    nc.vector.tensor_tensor(
+                        diff[:, li, cs].rearrange("p c (g w) -> p c g w", g=g),
+                        got[:, li, cs].rearrange("p c (g w) -> p c g w", g=g),
+                        plain[:, cs, :, j0 : j0 + width],
+                        ALU.subtract,
+                    )
+                if False:
+                    nc.scalar.activation(sq[:, li, 0], diff[:, li, 0], ACT.Square)
+                    nc.vector.tensor_tensor(sq[:, li, 1], diff[:, li, 1], diff[:, li, 1], ALU.mult)
+                else:
+                    nc.scalar.activation(sq[:, li], diff[:, li], ACT.Square)
             d, e, dp, ep = diff[:, 0, 0], diff[:, 0, 1], diff[:, 1, 0], diff[:, 1, 1]
-            q_bank = new_bank()
-            turn(q_bank, (sq[:, 1, 0], sq[:, 1, 1]), g)
-            r_bank = new_bank()
-            turn(r_bank, (sq[:, 0, 0], sq[:, 0, 1]), g)
-            d_bank = new_bank()
-            turn(d_bank, (d,), g)
-            n1 = work.tile([P, S], F32, name="n1")
-            n2 = work.tile([P, S], F32, name="n2")
-            n3 = work.tile([P, S], F32, name="n3")
+            q_bank = new_bank("qr")
+            r_bank = new_bank("qr")
+            q_t = turn(q_bank, (sq[:, 1, 0], sq[:, 1, 1]), g, width)
+            r_t = turn(r_bank, (sq[:, 0, 0], sq[:, 0, 1]), g, width)
+            n1 = work.tile([P, cols], F32, name="n1")
+            n2 = work.tile([P, cols], F32, name="n2")
+            n3 = work.tile([P, cols], F32, name="n3")
             nc.vector.tensor_tensor(n2[:], e, ep, ALU.mult)
             nc.vector.tensor_tensor(n1[:], d, sq[:, 1, 0], ALU.mult)
             nc.vector.tensor_tensor(n3[:], n2[:], dp, ALU.mult)
-            n_bank = new_bank()
-            turn(n_bank, (n1[:], n3[:]), g)
 
-            rho = work.tile([P, S], F32, name="rho")
-            den2 = work.tile([P, 2, S], F32, name="den2")
-            inv = work.tile([P, 2, S], F32, name="inv")
-            nc.scalar.activation(rho[:], q_bank[:], ACT.Abs_reciprocal_sqrt, bias=0.1)
-            nc.scalar.activation(den2[:, 0], r_bank[:], ACT.Square, scale=1.0 / 360.0, bias=1.0 / 9.0)
+            rho = work.tile([P, cols], F32, name="rho")
+            den2 = work.tile([P, 2, cols], F32, name="den2")
+            inv = work.tile([P, 2, cols], F32, name="inv")
+            nc.scalar.activation(by_slot(rho[:]), q_t, ACT.Abs_reciprocal_sqrt, bias=0.1)
+            nc.scalar.activation(by_slot(den2[:, 0]), r_t, ACT.Square, scale=1.0 / 360.0, bias=1.0 / 9.0)
+            n_t = turn(new_bank("mm") if lend else q_bank, (n1[:], n3[:]), g, width)
+            d_t = turn(new_bank("mm") if lend else r_bank, (d,), g, width)
             nc.scalar.activation(den2[:, 1], rho[:], ACT.Square, scale=0.18, bias=0.6)
             nc.scalar.activation(inv[:, 0], den2[:, 0], ACT.Abs_reciprocal_sqrt)
             nc.scalar.activation(inv[:, 1], den2[:, 1], ACT.Abs_reciprocal_sqrt)
-            rows = slice(j0 // P * PACK, (j0 + width) // P * PACK)
-            cols = slice(c0 // PACK, c0 // PACK + 32 * g)
-            for dst, k, const, bank in ((fene_t, 0, 10.0, d_bank), (bend_t, 1, 5.0 / 3.0, n_bank)):
-                nc.vector.scalar_tensor_tensor(
-                    dst[:, rows, cols],
-                    inv[:, k].rearrange("p (a m) -> p a m", m=32 * g),
-                    const,
-                    bank[:].rearrange("p (a m) -> p a m", m=32 * g),
-                    ALU.subtract,
-                    ALU.mult,
-                )
+            rows = slice(c0 // PACK, c0 // PACK + 32 * g)
+            for dst, k, const, factor in ((fene_t, 0, 10.0, d_t), (bend_t, 1, 5.0 / 3.0, n_t)):
+                for s0 in range(0, width, piece):
+                    nb = piece // P
+                    jb = (j0 + s0) // P
+                    part = slice(s0 // P * 32 * g, (s0 + piece) // P * 32 * g)
+                    nc.vector.scalar_tensor_tensor(
+                        dst[:, jb // 2, :, jb % 2 : jb % 2 + nb, rows],
+                        by_slot(inv[:, k])[:, :, part].rearrange("p t (b m) -> p t b m", b=nb),
+                        const,
+                        factor[:, :, part].rearrange("p t (b m) -> p t b m", b=nb),
+                        ALU.subtract,
+                        ALU.mult,
+                    )
+            return q_bank, r_bank
 
-        def observe(j0, width, w3_codes, w3_scales):
+        def observe(j0, width, w3_codes, w3_scales, banks):
             hid = work.tile([P, width, PACK], BF16, name="hid", align_bytes=64)
             for jb in range(j0 // P, (j0 + width) // P):
-                bank = new_bank()
-                for t in range(PACK):
-                    for n, term in enumerate((fene_t, bend_t)):
+                bank = banks[jb - j0 // P]
+                for n, term in enumerate((fene_t, bend_t)):
+                    for t in range(PACK):
                         nc.tensor.matmul(
-                            bank[:, t * P : (t + 1) * P], term[:, jb * PACK + t, :], ident[:],
-                            is_transpose=True, start=(n == 0), stop=(n == 1),
+                            bank[:, t * P : (t + 1) * P], term[:, jb // 2, t, jb % 2, :], ident[:],
+                            is_transpose=True, start=(n == 0 and t == 0), stop=(n == 1 and t == PACK - 1),
                         )
-                nc.vector.tensor_tensor(
+                nc.vector.scalar_tensor_tensor(
                     hid[:, jb * P - j0 : (jb + 1) * P - j0, :],
                     bank[:].rearrange("p (t j) -> p j t", t=PACK),
+                    -1.0,
                     unit_sb[:].unsqueeze(1).to_broadcast([P, P, PACK]),
+                    ALU.mult,
                     ALU.mult,
                 )
             codes = work.tile([P, width], U32, name="hid_codes", align_bytes=64)
@@ -201,7 +238,7 @@ def tile_picked_ypolym_force_p_kernel(
             nc.vector.quantize_mx(
                 out=codes[:].bitcast(FP8X4), scales=scales[:], in_=hid[:].rearrange("p j t -> p (j t)")
             )
-            bank = new_bank()
+            bank = new_bank("mm")
             nc.tensor.matmul_mx(
                 out=bank[:, :width], lhsT=w3_codes[:].bitcast(FP8X4), lhsT_scale=w3_scales[:],
                 rhs=codes[:].bitcast(FP8X4), rhs_scale=scales[:], start=True, stop=True,
@@ -212,11 +249,12 @@ def tile_picked_ypolym_force_p_kernel(
 
         xy0 = products(0)
         xy1 = products(1)
-        forces(0, xy0, 0)
+        forces(0, xy0, 0, 512, False)
         xy2 = products(2)
-        forces(1, xy1, 0)
-        w3_codes, w3_scales = quantise(w3_raw, N, False, "w3", False)
-        forces(2, xy2, 0)
-        observe(0, 256, w3_codes, w3_scales)
-        forces(2, xy2, 256)
-        observe(256, 256, w3_codes, w3_scales)
+        forces(1, xy1, 0, 512, False)
+        w3_codes, w3_scales = quantise(w3_raw, N, "w3", "V")
+        forces(2, xy2, 0, 256, False)
+        lent = forces(2, xy2, 256, 256, True)
+        observe(0, 256, w3_codes, w3_scales, lent)
+        observe(256, 128, w3_codes, w3_scales, [new_bank("qr")])
+        observe(384, 128, w3_codes, w3_scales, [new_bank("qr")])

@@ -41,6 +41,9 @@ def tile_picked_ypolym_force_p_kernel(
         all_scales = keep.tile([P, T], U8, name="all_scales", align_bytes=64)
         all_words = keep.tile([P, T], U32, name="all_words", align_bytes=64)
         nc.gpsimd.memset(all_scales[:].bitcast(I32), 0)
+        warm = keep.tile([P, 2], F32, name="warm")
+        nc.vector.memset(warm[:, 0:1], 1.0)
+        nc.scalar.activation(warm[:, 1:2], warm[:, 0:1], ACT.Abs_reciprocal_sqrt)
         nc.sync.dma_start(offs_sb[:], offs)
         for q in range(4):
             nc.sync.dma_start(
@@ -149,7 +152,7 @@ def tile_picked_ypolym_force_p_kernel(
             for li in (1, 0):
                 rest = []
                 for c in range(2):
-                    fused = c == 0 or gi == 2
+                    fused = c == 0 or (gi == 2 and (j0 > 0 or li == 0))
                     for pl in range(g):
                         for s0 in range(0, width, piece):
                             part = slice(pl * width + s0, pl * width + s0 + piece)
@@ -172,7 +175,7 @@ def tile_picked_ypolym_force_p_kernel(
                         plain[:, cs, :, j0 : j0 + width],
                         ALU.subtract,
                     )
-                if False:
+                if j0 >= 256:
                     nc.scalar.activation(sq[:, li, 0], diff[:, li, 0], ACT.Square)
                     nc.vector.tensor_tensor(sq[:, li, 1], diff[:, li, 1], diff[:, li, 1], ALU.mult)
                 else:

from contextlib import ExitStack

import concourse.mybir as mybir
from concourse.masks import make_identity

K, T, S, N, H = 512, 1024, 512, 128, 512
FLOPS = 2 * K * H * S * 2 + 2 * H * N * S

F32 = mybir.dt.float32
BF16 = mybir.dt.bfloat16
I32 = mybir.dt.int32
U32 = mybir.dt.uint32
U16 = mybir.dt.uint16
U8 = mybir.dt.uint8
FP8X4 = mybir.dt.float8_e4m3fn_x4
ALU = mybir.AluOpType
ACT = mybir.ActivationFunctionType

P = 128
PACK = 4
PIECE = 256
BANKS = {"mm":4,"qr":4}
GROUPS = ((0, 1), (128, 1), (256, 2))


def tile_picked_ypolym_force_p_kernel(
    tc, x_words, x_scales, w1, w2, unit, w3, offs, nxt, prv, out
):
    nc = tc.nc
    with ExitStack() as ctx:
        keep = ctx.enter_context(tc.tile_pool(name="keep", bufs=1))
        work = ctx.enter_context(tc.tile_pool(name="work", bufs=3))
        psum = ctx.enter_context(tc.psum_pool(name="psum", bufs=1))

        def new_bank(tag):
            return psum.tile([P, 512], F32, name=tag, tag=tag, bufs=BANKS[tag])

        offs_sb = keep.tile([P, S // 16], U16, name="offs_sb")
        nxt_sb = keep.tile([P, S // 16], U16, name="nxt_sb")
        prv_sb = keep.tile([P, S // 16], U16, name="prv_sb")
        all_scales = keep.tile([P, T], U8, name="all_scales", align_bytes=64)
        all_words = keep.tile([P, T], U32, name="all_words", align_bytes=64)
        nc.gpsimd.memset(all_scales[:].bitcast(I32), 0)
        warm = keep.tile([P, 2], F32, name="warm")
        nc.vector.memset(warm[:, 0:1], 1.0)
        nc.scalar.activation(warm[:, 1:2], warm[:, 0:1], ACT.Abs_reciprocal_sqrt)
        nc.sync.dma_start(offs_sb[:], offs)
        for q in range(4):
            nc.sync.dma_start(
                all_scales[32 * q : 32 * q + 4, :].bitcast(I32),
                x_scales[0, 4 * q : 4 * q + 4, :].bitcast(I32),
            )
        nc.sync.dma_start(
            all_words[:].bitcast(I32), x_words[0].rearrange("p n t -> p (n t)").bitcast(I32)
        )

        def load_w(w, c0, width, name):
            raw = keep.tile([P, PACK, width], F32, name=name)
            nc.sync.dma_start(raw[:], w[:, c0 : c0 + width].rearrange("(p j) c -> p j c", j=PACK))
            return raw

        raws = {}
        for gi, (c0, g) in enumerate(GROUPS):
            raws[gi] = (load_w(w1, c0, P * g, "w1_raw%d" % gi), load_w(w2, c0, P * g, "w2_raw%d" % gi))
            if gi == 0:
                nc.sync.dma_start(prv_sb[:], prv)
                nc.sync.dma_start(nxt_sb[:], nxt)
        w3_raw = load_w(w3, 0, N, "w3_raw")
        unit_sb = keep.tile([P, PACK], F32, name="unit_sb")
        nc.sync.dma_start(unit_sb[:], unit.rearrange("(p t) o -> p (t o)", t=PACK))
        lists = (nxt_sb, prv_sb)

        ident = keep.tile([P, P], F32, name="ident")
        make_identity(nc, ident[:])

        x_bytes = keep.tile([P, S], U8, name="x_bytes", align_bytes=64)
        x_codes = keep.tile([P, S], U32, name="x_codes", align_bytes=64)
        nc.vector.tensor_copy(x_bytes[:], all_scales[:].indirect(offs_sb[:]))
        nc.vector.tensor_copy(x_codes[:], all_words[:].indirect(offs_sb[:]))

        def quantise(raw, width, name, eng):
            wb = keep.tile([P, width * PACK], BF16, name=name + "_bf", align_bytes=64)
            dst = wb[:].rearrange("p (m t j) -> p m j t", t=PACK, j=PACK)
            src = raw[:].rearrange("p j (m t) -> p m j t", t=PACK)
            if eng == "S":
                nc.scalar.copy(dst, src)
            elif eng == "G":
                nc.gpsimd.tensor_scalar(
                    wb[:].rearrange("p (m j) -> p m j", j=PACK), raw[:].rearrange("p j m -> p m j"),
                    1.0, 0.0, ALU.mult, ALU.add,
                )
            else:
                nc.vector.tensor_copy(dst, src)
            codes = keep.tile([P, width], U32, name=name + "_codes", align_bytes=64)
            scales = keep.tile([P, width], U8, name=name + "_scales", align_bytes=64)
            nc.vector.quantize_mx(out=codes[:].bitcast(FP8X4), scales=scales[:], in_=wb[:])
            return codes, scales

        def products(gi):
            c0, g = GROUPS[gi]
            tables = [[], []]
            plain = keep.tile([P, 2, g, S], F32, name="plain%d" % gi)
            for c in range(2):
                codes, scales = quantise(raws[gi][c], P * g, "w%d_%d" % (c, gi), "SSVVVVVVV"[2 * gi + c])
                for pl in range(g):
                    bank = new_bank("mm")
                    cols = slice(pl * P, (pl + 1) * P)
                    nc.tensor.matmul_mx(
                        out=bank[:], lhsT=codes[:, cols].bitcast(FP8X4), lhsT_scale=scales[:, cols],
                        rhs=x_codes[:].bitcast(FP8X4), rhs_scale=x_bytes[:], start=True, stop=True,
                    )
                    if gi > 1 or c == 0:
                        table = keep.tile([P, S], F32, name="table%d_%d_%d" % (gi, c, pl))
                        nc.scalar.copy(table[:], bank[:])
                        if gi == 0:
                            nc.scalar.copy(plain[:, c, pl, :], bank[:])
                        else:
                            nc.sync.dma_start(plain[:, c, pl, :], table[:])
                        tables[c].append(table[:])
                    else:
                        nc.scalar.copy(plain[:, c, pl, :], bank[:])
                        tables[c].append(plain[:, c, pl, :])
            return tables, plain

        fene_t = keep.tile([P, 2, PACK, 2, P], F32, name="fene_t")
        bend_t = keep.tile([P, 2, PACK, 2, P], F32, name="bend_t")

        def turn(bank, terms, g, width):
            for jb in range(width // P):
                for pl in range(g):
                    dst = bank[:, (jb * g + pl) * P : (jb * g + pl + 1) * P]
                    cols = slice(pl * width + jb * P, pl * width + (jb + 1) * P)
                    for n, term in enumerate(terms):
                        nc.tensor.matmul(
                            dst, term[:, cols], ident[:], is_transpose=True,
                            start=(n == 0), stop=(n == len(terms) - 1),
                        )
            return bank[:, : g * width].rearrange("p (a t) -> p t a", t=PACK)

        def by_slot(ap):
            return ap.rearrange("p (t a) -> p t a", t=PACK)

        def forces(gi, made, j0, width, lend):
            tables, plain = made
            c0, g = GROUPS[gi]
            u = (gi, j0)
            cols = g * width
            piece = min(PIECE, width)
            got = work.tile([P, 2, 2, cols], F32, name="got")
            diff = work.tile([P, 2, 2, cols], F32, name="diff")
            sq = work.tile([P, 2, 2, cols], F32, name="sq")
            for li in (1, 0):
                rest = []
                for c in range(2):
                    fused = c == 0 or (gi == 2 and (j0 > 0 or li == 0))
                    for pl in range(g):
                        for s0 in range(0, width, piece):
                            part = slice(pl * width + s0, pl * width + s0 + piece)
                            src = tables[c][pl].indirect(lists[li][:, (j0 + s0) // 16 : (j0 + s0 + piece) // 16])
                            if fused:
                                nc.vector.tensor_tensor(
                                    diff[:, li, c, part], src, plain[:, c, pl, j0 + s0 : j0 + s0 + piece], ALU.subtract
                                )
                            elif c == 0:
                                nc.vector.tensor_copy(got[:, li, c, part], src)
                            else:
                                nc.scalar.activation(got[:, li, c, part], src, ACT.Copy)
                    if not fused:
                        rest.append(c)
                if rest:
                    cs = slice(rest[0], rest[-1] + 1)
                    nc.vector.tensor_tensor(
                        diff[:, li, cs].rearrange("p c (g w) -> p c g w", g=g),
                        got[:, li, cs].rearrange("p c (g w) -> p c g w", g=g),
                        plain[:, cs, :, j0 : j0 + width],
                        ALU.subtract,
                    )
                if j0 >= 256:
                    nc.scalar.activation(sq[:, li, 0], diff[:, li, 0], ACT.Square)
                    nc.vector.tensor_tensor(sq[:, li, 1], diff[:, li, 1], diff[:, li, 1], ALU.mult)
                else:
                    nc.scalar.activation(sq[:, li], diff[:, li], ACT.Square)
            d, e, dp, ep = diff[:, 0, 0], diff[:, 0, 1], diff[:, 1, 0], diff[:, 1, 1]
            q_bank = new_bank("qr")
            r_bank = new_bank("qr")
            q_t = turn(q_bank, (sq[:, 1, 0], sq[:, 1, 1]), g, width)
            r_t = turn(r_bank, (sq[:, 0, 0], sq[:, 0, 1]), g, width)
            n1 = work.tile([P, cols], F32, name="n1")
            n2 = work.tile([P, cols], F32, name="n2")
            n3 = work.tile([P, cols], F32, name="n3")
            nc.vector.tensor_tensor(n2[:], e, ep, ALU.mult)
            nc.vector.tensor_tensor(n1[:], d, sq[:, 1, 0], ALU.mult)
            nc.vector.tensor_tensor(n3[:], n2[:], dp, ALU.mult)

            rho = work.tile([P, cols], F32, name="rho")
            den2 = work.tile([P, 2, cols], F32, name="den2")
            inv = work.tile([P, 2, cols], F32, name="inv")
            nc.scalar.activation(by_slot(rho[:]), q_t, ACT.Abs_reciprocal_sqrt, bias=0.1)
            nc.scalar.activation(by_slot(den2[:, 0]), r_t, ACT.Square, scale=1.0 / 360.0, bias=1.0 / 9.0)
            n_t = turn(new_bank("mm") if lend else q_bank, (n1[:], n3[:]), g, width)
            d_t = turn(new_bank("mm") if lend else r_bank, (d,), g, width)
            nc.scalar.activation(den2[:, 1], rho[:], ACT.Square, scale=0.18, bias=0.6)
            nc.scalar.activation(inv[:, 0], den2[:, 0], ACT.Abs_reciprocal_sqrt)
            nc.scalar.activation(inv[:, 1], den2[:, 1], ACT.Abs_reciprocal_sqrt)
            rows = slice(c0 // PACK, c0 // PACK + 32 * g)
            for dst, k, const, factor in ((fene_t, 0, 10.0, d_t), (bend_t, 1, 5.0 / 3.0, n_t)):
                for s0 in range(0, width, piece):
                    nb = piece // P
                    jb = (j0 + s0) // P
                    part = slice(s0 // P * 32 * g, (s0 + piece) // P * 32 * g)
                    nc.vector.scalar_tensor_tensor(
                        dst[:, jb // 2, :, jb % 2 : jb % 2 + nb, rows],
                        by_slot(inv[:, k])[:, :, part].rearrange("p t (b m) -> p t b m", b=nb),
                        const,
                        factor[:, :, part].rearrange("p t (b m) -> p t b m", b=nb),
                        ALU.subtract,
                        ALU.mult,
                    )
            return q_bank, r_bank

        def observe(j0, width, w3_codes, w3_scales, banks):
            hid = work.tile([P, width, PACK], BF16, name="hid", align_bytes=64)
            for jb in range(j0 // P, (j0 + width) // P):
                bank = banks[jb - j0 // P]
                for n, term in enumerate((fene_t, bend_t)):
                    for t in range(PACK):
                        nc.tensor.matmul(
                            bank[:, t * P : (t + 1) * P], term[:, jb // 2, t, jb % 2, :], ident[:],
                            is_transpose=True, start=(n == 0 and t == 0), stop=(n == 1 and t == PACK - 1),
                        )
                nc.vector.scalar_tensor_tensor(
                    hid[:, jb * P - j0 : (jb + 1) * P - j0, :],
                    bank[:].rearrange("p (t j) -> p j t", t=PACK),
                    -1.0,
                    unit_sb[:].unsqueeze(1).to_broadcast([P, P, PACK]),
                    ALU.mult,
                    ALU.mult,
                )
            codes = work.tile([P, width], U32, name="hid_codes", align_bytes=64)
            scales = work.tile([P, width], U8, name="hid_scales", align_bytes=64)
            nc.vector.quantize_mx(
                out=codes[:].bitcast(FP8X4), scales=scales[:], in_=hid[:].rearrange("p j t -> p (j t)")
            )
            bank = new_bank("mm")
            nc.tensor.matmul_mx(
                out=bank[:, :width], lhsT=w3_codes[:].bitcast(FP8X4), lhsT_scale=w3_scales[:],
                rhs=codes[:].bitcast(FP8X4), rhs_scale=scales[:], start=True, stop=True,
            )
            res = work.tile([P, width], F32, name="res")
            nc.scalar.copy(res[:], bank[:, :width])
            nc.sync.dma_start(out[:, j0 : j0 + width], res[:])

        xy0 = products(0)
        xy1 = products(1)
        forces(0, xy0, 0, 512, False)
        xy2 = products(2)
        forces(1, xy1, 0, 512, False)
        w3_codes, w3_scales = quantise(w3_raw, N, "w3", "V")
        forces(2, xy2, 0, 256, False)
        lent = forces(2, xy2, 256, 256, True)
        observe(0, 256, w3_codes, w3_scales, lent)
        observe(256, 128, w3_codes, w3_scales, [new_bank("qr")])
        observe(384, 128, w3_codes, w3_scales, [new_bank("qr")])
